import numpy as np
import ml_dtypes


def mxq(x, axis, fmt="e4m3"):
    dtype, down = {"e4m3": (ml_dtypes.float8_e4m3fn, 7), "e5m2": (ml_dtypes.float8_e5m2, 14)}[fmt]
    v = np.moveaxis(np.asarray(x, np.float32).astype(ml_dtypes.bfloat16).astype(np.float64), axis, -1)
    blocks = v.reshape(v.shape[:-1] + (-1, 32))
    amax = np.abs(blocks).max(-1, keepdims=True)
    byte = np.maximum(np.where(amax > 0, np.frexp(amax)[1] - 1 + 127, 0) - down, 1)
    scale = np.exp2(byte - 127.0)
    codes = (blocks / scale).astype(np.float32).astype(dtype).astype(np.float64)
    return np.moveaxis((codes * scale).reshape(v.shape), -1, axis)


WIDE = False


def mx_kscale(k):
    if not WIDE:
        return np.ones(k)
    levels = np.array([10, -10, 5, -5, 0])
    if k % 512:
        return np.exp2(np.random.permutation(np.resize(levels, k // 32))).repeat(32)
    a = np.empty((k // 512, 16))
    for p in range(k // 512):
        a[p, :8] = np.random.permutation(np.resize(levels, 8))
        for g in range(8):
            far = levels[np.abs(levels - a[p, g]) >= 10]
            a[p, g + 8] = far[np.random.randint(len(far))]
    return np.exp2(a.ravel()).repeat(32)


def f64(x):
    return np.asarray(x).astype(np.float64)


def striped(idx):
    return np.tile(np.asarray(idx).reshape(-1, 16).T, (8, 1)).astype(np.uint16)


def unstriped(offs):
    return offs[:16].T.reshape(-1).astype(np.int64)


E2M1 = np.array([0.0, 0.5, 1.0, 1.5, 2.0, 3.0, 4.0, 6.0, -0.0, -0.5, -1.0, -1.5, -2.0, -3.0, -4.0, -6.0])


def pack_weight(w, fmt):
    k, n = w.shape
    w = f64(np.asarray(w, np.float32).astype(ml_dtypes.bfloat16)).reshape(k // 32, 32, n)
    amax = np.abs(w).max(1)
    if fmt == "e4m3":
        byte = np.frexp(amax)[1] - 1 + 127 - 7
    else:
        mant, ex = np.frexp(amax / 6.0)
        byte = np.where(mant > 0.5, ex, ex - 1) + 127
    byte = np.clip(np.where(amax > 0, byte, 1), 1, 254)
    scaled = (w * np.exp2(127.0 - byte)[:, None, :]).reshape(k, n).astype(np.float32)
    by_word = np.ascontiguousarray(scaled.reshape(k // 512, 128, 4, n).transpose(0, 1, 3, 2))
    if fmt == "e4m3":
        words = by_word.astype(ml_dtypes.float8_e4m3fn).view(np.uint8)
    else:
        c = by_word.astype(ml_dtypes.float4_e2m1fn).view(np.uint8) & 0xF
        words = (c[..., 0::2] | (c[..., 1::2] << 4)).reshape(k // 512, 128, 2 * n)
    return np.ascontiguousarray(words), np.ascontiguousarray(byte.astype(np.uint8).reshape(k // 512, 16, n))


def unpack_weight(words, scales, fmt):
    g, _, n = scales.shape
    words = np.ascontiguousarray(words).reshape(g, 128, n, -1)
    if fmt == "e4m3":
        vals = words.view(ml_dtypes.float8_e4m3fn).astype(np.float64)
    else:
        nib = np.empty((g, 128, n, 4), np.uint8)
        nib[..., 0::2] = words & 0xF
        nib[..., 1::2] = words >> 4
        vals = E2M1[nib]
    vals = vals * np.repeat(np.exp2(scales.astype(np.float64) - 127.0), 8, axis=1)[..., None]
    return vals.transpose(0, 1, 3, 2).reshape(g * 512, n)


D, T, I, Q, E, M = 512, 1024, 512, 512, 512, 1024


def setup_inputs():
    n = np.random.standard_normal
    idx = np.random.permutation(T)[:I]
    idx2 = np.random.permutation(T)[:I]
    idx3 = np.random.permutation(T)[:I]
    idx4 = np.random.permutation(M)[:I]
    fd = mx_kscale(D)
    fq = mx_kscale(Q)
    keysp = pack_weight(n((D, T)) / fd[:, None], "e4m3")
    return {
        "query": (n((D, Q)) * 1.0 / np.sqrt(D) * fd[:, None]).astype(np.float32),
        "keys_words": keysp[0],
        "keys_scales": keysp[1],
        "lam": (np.random.uniform(0.4, 1.0, (Q, 1))).astype(np.float32),
        "qs": (np.random.uniform(0.5, 2.0, (Q, 1)) * fq[:, None]).astype(np.float32),
        "msgs": (n((Q, E)) * 1 / np.sqrt(Q) / fq[:, None]).astype(np.float32),
        "old": (n((E, M)) * 1.0).astype(np.float32),
        "offs": striped(idx),
        "offs2": striped(idx2),
        "offs3": striped(idx3),
        "offs4": striped(idx4),
    }


def reference(query, keys_words, keys_scales, lam, qs, msgs, old, offs, offs2, offs3, offs4):
    idx = unstriped(offs)
    idx2 = unstriped(offs2)
    idx3 = unstriped(offs3)
    idx4 = unstriped(offs4)
    keysu = unpack_weight(keys_words, keys_scales, "e4m3")
    queryq = mxq(f64(query), 0, "e4m3")
    a = queryq.T @ keysu
    w = a[:, idx] + np.tanh(a[:, idx2] - a[:, idx3]) * f64(lam)
    wq = w * f64(qs)
    msgsq = mxq(f64(msgs), 0, "e4m3")
    wqq = mxq(wq, 0, "e4m3")
    dl = msgsq.T @ wqq
    df = np.zeros((E, M))
    df[:, idx4] = dl
    y = f64(old) + df
    return y

@@ -1,0 +1,222 @@
+from contextlib import ExitStack
+
+import concourse.mybir as mybir
+
+D, T, I, Q, E, M = 512, 1024, 512, 512, 512, 1024
+FLOPS = 2 * D * Q * T + 2 * Q * E * I
+
+F32 = mybir.dt.float32
+BF16 = mybir.dt.bfloat16
+I32 = mybir.dt.int32
+U32 = mybir.dt.uint32
+U16 = mybir.dt.uint16
+U8 = mybir.dt.uint8
+FP8X4 = mybir.dt.float8_e4m3fn_x4
+ALU = mybir.AluOpType
+ACT = mybir.ActivationFunctionType
+
+P = 128
+PACK = 4
+BANK = 512
+HALVES = 2
+HS = I // HALVES
+HC = HS // 16
+
+
+def tile_attend_seconded_deliveredplanes_lean_kernel(
+    tc, query, keys_words, keys_scales, lam, qs, msgs, old, offs, offs2, offs3, offs4, out
+):
+    nc = tc.nc
+    with ExitStack() as ctx:
+        keep = ctx.enter_context(tc.tile_pool(name="keep", bufs=1))
+        psum_a = ctx.enter_context(tc.psum_pool(name="psum_a", bufs=4))
+        psum_d = ctx.enter_context(tc.psum_pool(name="psum_d", bufs=4))
+
+        def sb(name, shape, dtype):
+            return keep.tile(shape, dtype, name=name, align_bytes=64)
+
+        lists = {n: keep.tile([P, I // 16], U16, name=n) for n in ("own", "sec", "opp", "dst")}
+        q_raw = [sb(f"q_raw{c}", [P, PACK, Q // 2], F32) for c in range(2)]
+        k_words = [sb(f"k_words{c}", [P, BANK], U32) for c in range(T // BANK)]
+        k_scales = sb("k_scales", [P, T], U8)
+        lam_t = sb("lam_t", [P, PACK], F32)
+        qs_t = sb("qs_t", [P, PACK], F32)
+        m_raw = sb("m_raw", [P, PACK, E], F32)
+        old_t = [sb(f"old{u}", [P, M], F32) for u in range(E // P)]
+        df = [sb(f"df{u}", [P, M], F32) for u in range(E // P)]
+
+        nc.vector.memset(k_scales[:].bitcast(I32), 0)
+        q_view = query.rearrange("(p j) q -> p j q", j=PACK)
+        for c in range(2):
+            nc.sync.dma_start(out=q_raw[c][:], in_=q_view[:, :, c * (Q // 2) : (c + 1) * (Q // 2)])
+        for g in range(4):
+            nc.sync.dma_start(
+                out=k_scales[32 * g : 32 * g + 4, :].bitcast(I32),
+                in_=keys_scales[0, 4 * g : 4 * g + 4, :].bitcast(I32),
+            )
+        kw = keys_words[0].rearrange("p n r -> p (n r)")
+        for c in range(T // BANK):
+            nc.sync.dma_start(
+                out=k_words[c][:].bitcast(I32),
+                in_=kw[:, c * BANK * PACK : (c + 1) * BANK * PACK].bitcast(I32),
+            )
+        nc.gpsimd.dma_start(out=qs_t[:], in_=qs.rearrange("(p t) o -> p (t o)", t=PACK))
+        nc.gpsimd.dma_start(out=lam_t[:], in_=lam.rearrange("(p t) o -> p (t o)", t=PACK))
+        nc.sync.dma_start(lists["opp"][:], offs3)
+        nc.sync.dma_start(lists["own"][:], offs)
+        nc.sync.dma_start(lists["sec"][:], offs2)
+        nc.sync.dma_start(out=m_raw[:], in_=msgs.rearrange("(p j) e -> p j e", j=PACK))
+        nc.sync.dma_start(lists["dst"][:], offs4)
+        for u in range(E // P):
+            nc.sync.dma_start(out=old_t[u][:], in_=old[u * P : (u + 1) * P, :])
+        for u in range(E // P):
+            nc.vector.memset(df[u][:], 0.0)
+
+        qs_wide = sb("qs_wide", [P, PACK, HS], F32)
+        for t in range(PACK):
+            nc.vector.tensor_copy(out=qs_wide[:, t, :], in_=qs_t[:, t : t + 1].to_broadcast([P, HS]))
+        lq = sb("lq", [P, PACK], F32)
+        nc.vector.tensor_tensor(out=lq[:], in0=lam_t[:], in1=qs_t[:], op=ALU.mult)
+
+        q_bf = sb("q_bf", [P, PACK, P, PACK], BF16)
+        for c in range(2):
+            nc.vector.tensor_copy(
+                out=q_bf[:, :, c * (P // 2) : (c + 1) * (P // 2), :].rearrange("p t m j -> p m t j"),
+                in_=q_raw[c][:].rearrange("p j (m t) -> p m t j", t=PACK),
+            )
+        q_codes = [sb(f"q_codes{t}", [P, P], U32) for t in range(PACK)]
+        q_scales = [sb(f"q_scales{t}", [P, P], U8) for t in range(PACK)]
+        for t in range(PACK):
+            nc.vector.quantize_mx(
+                out=q_codes[t][:].bitcast(FP8X4),
+                scales=q_scales[t][:],
+                in_=q_bf[:, t, :, :].rearrange("p m j -> p (m j)"),
+            )
+
+        a = [sb(f"a{t}", [P, T], F32) for t in range(PACK)]
+
+        def scores(t):
+            for c in range(T // BANK):
+                cols = slice(c * BANK, (c + 1) * BANK)
+                bank = psum_a.tile([P, BANK], F32, name="a_bank")
+                nc.tensor.matmul_mx(
+                    out=bank[:],
+                    lhsT=q_codes[t][:].bitcast(FP8X4),
+                    lhsT_scale=q_scales[t][:],
+                    rhs=k_words[c][:].bitcast(FP8X4),
+                    rhs_scale=k_scales[:, cols],
+                    start=True,
+                    stop=True,
+                )
+                if t == 0 and c == 1:
+                    nc.vector.tensor_copy(out=a[t][:, cols], in_=bank[:])
+                else:
+                    nc.scalar.copy(out=a[t][:, cols], in_=bank[:])
+
+        wq_bf = [sb(f"wq_bf{h}", [P, PACK, HS], BF16) for h in range(HALVES)]
+
+        def weights(t, h):
+            lc = slice(h * HC, (h + 1) * HC)
+            opp = sb(f"opp{t}{h}", [P, HS], F32)
+            nc.scalar.activation(opp[:], a[t][:].indirect(lists["opp"][:, lc]), ACT.Copy)
+            own = sb(f"own{t}{h}", [P, HS], F32)
+            nc.vector.tensor_tensor(own[:], a[t][:].indirect(lists["own"][:, lc]), qs_wide[:, t, :], ALU.mult)
+            diff = sb(f"diff{t}{h}", [P, HS], F32)
+            nc.vector.tensor_tensor(diff[:], a[t][:].indirect(lists["sec"][:, lc]), opp[:], ALU.subtract)
+            th = sb(f"th{t}{h}", [P, HS], F32)
+            nc.scalar.activation(th[:], diff[:], ACT.Tanh)
+            return th, own
+
+        def combine(t, h, th, own):
+            nc.vector.scalar_tensor_tensor(
+                out=wq_bf[h][:, t, :], in0=th[:], scalar=lq[:, t : t + 1], in1=own[:], op0=ALU.mult, op1=ALU.add
+            )
+
+        m_codes = sb("m_codes", [P, E], U32)
+        m_scales = sb("m_scales", [P, E], U8)
+
+        def messages():
+            m_bf = sb("m_bf", [P, E, PACK], BF16)
+            nc.vector.tensor_copy(
+                out=m_bf[:].rearrange("p (c i) j -> p c j i", i=4),
+                in_=m_raw[:].rearrange("p j (c i) -> p c j i", i=4),
+            )
+            nc.vector.quantize_mx(
+                out=m_codes[:].bitcast(FP8X4), scales=m_scales[:], in_=m_bf[:].rearrange("p e j -> p (e j)")
+            )
+
+        def deliver(h):
+            wq_il = sb(f"wq_il{h}", [P, HS, PACK], BF16)
+            nc.vector.tensor_copy(
+                out=wq_il[:].rearrange("p (c i) t -> p c t i", i=4),
+                in_=wq_bf[h][:].rearrange("p t (c i) -> p c t i", i=4),
+            )
+            w_codes = sb(f"w_codes{h}", [P, HS], U32)
+            w_scales = sb(f"w_scales{h}", [P, HS], U8)
+            nc.vector.quantize_mx(
+                out=w_codes[:].bitcast(FP8X4), scales=w_scales[:], in_=wq_il[:].rearrange("p i t -> p (i t)")
+            )
+            banks = []
+            for v in range(2):
+                bank = psum_d.tile([P, 2, HS], F32, name="d_bank")
+                for s in range(2):
+                    cols = slice((2 * v + s) * P, (2 * v + s + 1) * P)
+                    nc.tensor.matmul_mx(
+                        out=bank[:, s, :],
+                        lhsT=m_codes[:, cols].bitcast(FP8X4),
+                        lhsT_scale=m_scales[:, cols],
+                        rhs=w_codes[:].bitcast(FP8X4),
+                        rhs_scale=w_scales[:],
+                        start=True,
+                        stop=True,
+                    )
+                banks.append(bank)
+            return banks
+
+        def unload(h, v, bank, on_vector):
+            dl = sb(f"dl{h}{v}", [P, 2, HS], F32)
+            if on_vector:
+                nc.vector.tensor_copy(out=dl[:], in_=bank[:])
+            else:
+                nc.scalar.copy(out=dl[:], in_=bank[:])
+            return dl
+
+        def place(u, h, src, on_vector):
+            window = df[u][:].indirect(lists["dst"][:, h * HC : (h + 1) * HC])
+            if on_vector:
+                nc.vector.tensor_copy(window, src)
+            else:
+                nc.scalar.activation(window, src, ACT.Copy)
+
+        def finish(u):
+            for c in range(2):
+                cols = slice(c * BANK, (c + 1) * BANK)
+                nc.vector.tensor_tensor(out=old_t[u][:, cols], in0=old_t[u][:, cols], in1=df[u][:, cols], op=ALU.add)
+                nc.sync.dma_start(out=out[u * P : (u + 1) * P, cols], in_=old_t[u][:, cols])
+
+        scores(0)
+        pending = None
+        for t in range(PACK):
+            parts = weights(t, 0)
+            if t + 1 < PACK:
+                scores(t + 1)
+            if pending is not None:
+                combine(t - 1, 0, *pending)
+            pending = parts
+            if t == 1:
+                messages()
+        second = [weights(0, 1)]
+        combine(PACK - 1, 0, *pending)
+        banks0 = deliver(0)
+        for t in range(1, PACK):
+            second.append(weights(t, 1))
+            combine(t - 1, 1, *second[t - 1])
+        dl0 = [unload(0, v, banks0[v], False) for v in range(2)]
+        combine(PACK - 1, 1, *second[PACK - 1])
+        banks1 = deliver(1)
+        for u in range(E // P):
+            place(u, 0, dl0[u // 2][:, u % 2, :], False)
+        dl1 = [unload(1, v, banks1[v], v == 0) for v in range(2)]
+        for u in range(E // P):
+            place(u, 1, dl1[u // 2][:, u % 2, :], u < 2)
+            finish(u)

@@ -32,8 +32,8 @@ def tile_attend_seconded_deliveredplanes_lean_kernel(
         psum_a = ctx.enter_context(tc.psum_pool(name="psum_a", bufs=4))
         psum_d = ctx.enter_context(tc.psum_pool(name="psum_d", bufs=4))
 
-        def sb(name, shape, dtype):
-            return keep.tile(shape, dtype, name=name, align_bytes=64)
+        def sb(name, shape, dtype, tag=None):
+            return keep.tile(shape, dtype, name=name, tag=tag or name, align_bytes=64)
 
         lists = {n: keep.tile([P, I // 16], U16, name=n) for n in ("own", "sec", "opp", "dst")}
         q_raw = [sb(f"q_raw{c}", [P, PACK, Q // 2], F32) for c in range(2)]
@@ -43,14 +43,14 @@ def tile_attend_seconded_deliveredplanes_lean_kernel(
         qs_t = sb("qs_t", [P, PACK], F32)
         m_raw = sb("m_raw", [P, PACK, E], F32)
         old_t = [sb(f"old{u}", [P, M], F32) for u in range(E // P)]
-        df = [sb(f"df{u}", [P, M], F32) for u in range(E // P)]
+        df = [sb(f"df{u}", [P, M], F32) for u in range(2)]
 
-        nc.vector.memset(k_scales[:].bitcast(I32), 0)
         q_view = query.rearrange("(p j) q -> p j q", j=PACK)
         for c in range(2):
             nc.sync.dma_start(out=q_raw[c][:], in_=q_view[:, :, c * (Q // 2) : (c + 1) * (Q // 2)])
+        nc.scalar.dma_start(out=qs_t[:], in_=qs.rearrange("(p t) o -> p (t o)", t=PACK))
         for g in range(4):
-            nc.sync.dma_start(
+            nc.scalar.dma_start(
                 out=k_scales[32 * g : 32 * g + 4, :].bitcast(I32),
                 in_=keys_scales[0, 4 * g : 4 * g + 4, :].bitcast(I32),
             )
@@ -60,7 +60,6 @@ def tile_attend_seconded_deliveredplanes_lean_kernel(
                 out=k_words[c][:].bitcast(I32),
                 in_=kw[:, c * BANK * PACK : (c + 1) * BANK * PACK].bitcast(I32),
             )
-        nc.gpsimd.dma_start(out=qs_t[:], in_=qs.rearrange("(p t) o -> p (t o)", t=PACK))
         nc.gpsimd.dma_start(out=lam_t[:], in_=lam.rearrange("(p t) o -> p (t o)", t=PACK))
         nc.sync.dma_start(lists["opp"][:], offs3)
         nc.sync.dma_start(lists["own"][:], offs)
@@ -69,28 +68,30 @@ def tile_attend_seconded_deliveredplanes_lean_kernel(
         nc.sync.dma_start(lists["dst"][:], offs4)
         for u in range(E // P):
             nc.sync.dma_start(out=old_t[u][:], in_=old[u * P : (u + 1) * P, :])
-        for u in range(E // P):
-            nc.vector.memset(df[u][:], 0.0)
+        for u in range(2):
+            nc.vector.memset(df[u][:].bitcast(I32), 0)
 
         qs_wide = sb("qs_wide", [P, PACK, HS], F32)
-        for t in range(PACK):
-            nc.vector.tensor_copy(out=qs_wide[:, t, :], in_=qs_t[:, t : t + 1].to_broadcast([P, HS]))
+        nc.vector.tensor_copy(out=qs_wide[:], in_=qs_t[:].unsqueeze(2).to_broadcast([P, PACK, HS]))
         lq = sb("lq", [P, PACK], F32)
-        nc.vector.tensor_tensor(out=lq[:], in0=lam_t[:], in1=qs_t[:], op=ALU.mult)
+        nc.gpsimd.tensor_tensor(out=lq[:], in0=lam_t[:], in1=qs_t[:], op=ALU.mult)
 
-        q_bf = sb("q_bf", [P, PACK, P, PACK], BF16)
+        q_bf = [sb(f"q_bf{t}", [P, P, PACK], BF16) for t in range(PACK)]
         for c in range(2):
-            nc.vector.tensor_copy(
-                out=q_bf[:, :, c * (P // 2) : (c + 1) * (P // 2), :].rearrange("p t m j -> p m t j"),
-                in_=q_raw[c][:].rearrange("p j (m t) -> p m t j", t=PACK),
-            )
+            for t in range(PACK):
+                dst = q_bf[t][:, c * (P // 2) : (c + 1) * (P // 2), :]
+                src = q_raw[c][:].rearrange("p j (m t) -> p t m j", t=PACK)[:, t, :, :]
+                if t % 2 == 0:
+                    nc.vector.tensor_copy(out=dst, in_=src)
+                else:
+                    nc.scalar.copy(out=dst, in_=src)
         q_codes = [sb(f"q_codes{t}", [P, P], U32) for t in range(PACK)]
         q_scales = [sb(f"q_scales{t}", [P, P], U8) for t in range(PACK)]
         for t in range(PACK):
             nc.vector.quantize_mx(
                 out=q_codes[t][:].bitcast(FP8X4),
                 scales=q_scales[t][:],
-                in_=q_bf[:, t, :, :].rearrange("p m j -> p (m j)"),
+                in_=q_bf[t][:].rearrange("p m j -> p (m j)"),
             )
 
         a = [sb(f"a{t}", [P, T], F32) for t in range(PACK)]
@@ -108,48 +109,59 @@ def tile_attend_seconded_deliveredplanes_lean_kernel(
                     start=True,
                     stop=True,
                 )
-                if t == 0 and c == 1:
+                if t < 2 and c == 1:
                     nc.vector.tensor_copy(out=a[t][:, cols], in_=bank[:])
                 else:
                     nc.scalar.copy(out=a[t][:, cols], in_=bank[:])
 
-        wq_bf = [sb(f"wq_bf{h}", [P, PACK, HS], BF16) for h in range(HALVES)]
+        def listed(name, t, h):
+            return a[t][:].indirect(lists[name][:, h * HC : (h + 1) * HC])
 
-        def weights(t, h):
-            lc = slice(h * HC, (h + 1) * HC)
-            opp = sb(f"opp{t}{h}", [P, HS], F32)
-            nc.scalar.activation(opp[:], a[t][:].indirect(lists["opp"][:, lc]), ACT.Copy)
-            own = sb(f"own{t}{h}", [P, HS], F32)
-            nc.vector.tensor_tensor(own[:], a[t][:].indirect(lists["own"][:, lc]), qs_wide[:, t, :], ALU.mult)
-            diff = sb(f"diff{t}{h}", [P, HS], F32)
-            nc.vector.tensor_tensor(diff[:], a[t][:].indirect(lists["sec"][:, lc]), opp[:], ALU.subtract)
+        def opponents(t, h, tag=None):
+            opp = sb(f"opp{t}{h}", [P, HS], F32, tag)
+            nc.scalar.activation(opp[:], listed("opp", t, h), ACT.Copy)
+            return opp
+
+        def owns(t, h, tag=None):
+            own = sb(f"own{t}{h}", [P, HS], F32, tag)
+            nc.vector.tensor_tensor(own[:], listed("own", t, h), qs_wide[:, t, :], ALU.mult)
+            return own
+
+        def contest(t, h, opp, diff):
+            nc.vector.tensor_tensor(diff, listed("sec", t, h), opp[:], ALU.subtract)
             th = sb(f"th{t}{h}", [P, HS], F32)
-            nc.scalar.activation(th[:], diff[:], ACT.Tanh)
-            return th, own
+            nc.scalar.activation(th[:], diff, ACT.Tanh)
+            return th
 
-        def combine(t, h, th, own):
+        def combine(t, wq_bf, th, own):
             nc.vector.scalar_tensor_tensor(
-                out=wq_bf[h][:, t, :], in0=th[:], scalar=lq[:, t : t + 1], in1=own[:], op0=ALU.mult, op1=ALU.add
+                out=wq_bf[:, t, :], in0=th, scalar=lq[:, t : t + 1], in1=own[:], op0=ALU.mult, op1=ALU.add
             )
 
         m_codes = sb("m_codes", [P, E], U32)
         m_scales = sb("m_scales", [P, E], U8)
 
-        def messages():
-            m_bf = sb("m_bf", [P, E, PACK], BF16)
-            nc.vector.tensor_copy(
-                out=m_bf[:].rearrange("p (c i) j -> p c j i", i=4),
-                in_=m_raw[:].rearrange("p j (c i) -> p c j i", i=4),
-            )
+        def round_messages(c, tag, on_vector):
+            m_bf = sb(f"m_bf{c}", [P, E // 2, PACK], BF16, tag)
+            dst = m_bf[:].rearrange("p (c i) j -> p c j i", i=4)
+            src = m_raw[:, :, c * (E // 2) : (c + 1) * (E // 2)].rearrange("p j (c i) -> p c j i", i=4)
+            if on_vector:
+                nc.vector.tensor_copy(out=dst, in_=src)
+            else:
+                nc.scalar.copy(out=dst, in_=src)
+            return m_bf
+
+        def quantise_messages(c, m_bf):
+            cols = slice(c * (E // 2), (c + 1) * (E // 2))
             nc.vector.quantize_mx(
-                out=m_codes[:].bitcast(FP8X4), scales=m_scales[:], in_=m_bf[:].rearrange("p e j -> p (e j)")
+                out=m_codes[:, cols].bitcast(FP8X4), scales=m_scales[:, cols], in_=m_bf[:].rearrange("p e j -> p (e j)")
             )
 
-        def deliver(h):
+        def deliver(h, wq_bf, order):
             wq_il = sb(f"wq_il{h}", [P, HS, PACK], BF16)
             nc.vector.tensor_copy(
                 out=wq_il[:].rearrange("p (c i) t -> p c t i", i=4),
-                in_=wq_bf[h][:].rearrange("p t (c i) -> p c t i", i=4),
+                in_=wq_bf[:].rearrange("p t (c i) -> p c t i", i=4),
             )
             w_codes = sb(f"w_codes{h}", [P, HS], U32)
             w_scales = sb(f"w_scales{h}", [P, HS], U8)
@@ -160,7 +172,8 @@ def tile_attend_seconded_deliveredplanes_lean_kernel(
             for v in range(2):
                 bank = psum_d.tile([P, 2, HS], F32, name="d_bank")
                 for s in range(2):
-                    cols = slice((2 * v + s) * P, (2 * v + s + 1) * P)
+                    u = order[2 * v + s]
+                    cols = slice(u * P, (u + 1) * P)
                     nc.tensor.matmul_mx(
                         out=bank[:, s, :],
                         lhsT=m_codes[:, cols].bitcast(FP8X4),
@@ -173,14 +186,6 @@ def tile_attend_seconded_deliveredplanes_lean_kernel(
                 banks.append(bank)
             return banks
 
-        def unload(h, v, bank, on_vector):
-            dl = sb(f"dl{h}{v}", [P, 2, HS], F32)
-            if on_vector:
-                nc.vector.tensor_copy(out=dl[:], in_=bank[:])
-            else:
-                nc.scalar.copy(out=dl[:], in_=bank[:])
-            return dl
-
         def place(u, h, src, on_vector):
             window = df[u][:].indirect(lists["dst"][:, h * HC : (h + 1) * HC])
             if on_vector:
@@ -188,35 +193,67 @@ def tile_attend_seconded_deliveredplanes_lean_kernel(
             else:
                 nc.scalar.activation(window, src, ACT.Copy)
 
-        def finish(u):
-            for c in range(2):
-                cols = slice(c * BANK, (c + 1) * BANK)
+        def finish(u, pieces):
+            for c in range(pieces):
+                cols = slice(c * M // pieces, (c + 1) * M // pieces)
                 nc.vector.tensor_tensor(out=old_t[u][:, cols], in0=old_t[u][:, cols], in1=df[u][:, cols], op=ALU.add)
                 nc.sync.dma_start(out=out[u * P : (u + 1) * P, cols], in_=old_t[u][:, cols])
 
+        wq0 = sb("wq_bf0", [P, PACK, HS], BF16)
         scores(0)
         pending = None
         for t in range(PACK):
-            parts = weights(t, 0)
+            opp = opponents(t, 0)
+            own = owns(t, 0)
             if t + 1 < PACK:
                 scores(t + 1)
+            diff = sb(f"diff{t}0", [P, HS], F32)
+            th = contest(t, 0, opp, diff[:])
             if pending is not None:
-                combine(t - 1, 0, *pending)
-            pending = parts
-            if t == 1:
-                messages()
-        second = [weights(0, 1)]
-        combine(PACK - 1, 0, *pending)
-        banks0 = deliver(0)
-        for t in range(1, PACK):
-            second.append(weights(t, 1))
-            combine(t - 1, 1, *second[t - 1])
-        dl0 = [unload(0, v, banks0[v], False) for v in range(2)]
-        combine(PACK - 1, 1, *second[PACK - 1])
-        banks1 = deliver(1)
-        for u in range(E // P):
-            place(u, 0, dl0[u // 2][:, u % 2, :], False)
-        dl1 = [unload(1, v, banks1[v], v == 0) for v in range(2)]
-        for u in range(E // P):
-            place(u, 1, dl1[u // 2][:, u % 2, :], u < 2)
-            finish(u)
+                combine(t - 1, wq0, *pending)
+            pending = (th[:], own)
+            if t == 2:
+                m_low = round_messages(0, "own10", True)
+            if t == 3:
+                quantise_messages(0, m_low)
+                quantise_messages(1, round_messages(1, "opp20", False))
+        combine(PACK - 1, wq0, *pending)
+        for c in range(2):
+            df.append(sb(f"df{2 + c}", [P, M], F32, f"k_words{c}"))
+            nc.gpsimd.memset(df[2 + c][:], 0.0)
+        banks0 = deliver(0, wq0, (0, 1, 2, 3))
+        opps = [opponents(t, 1, tag) for t, tag in enumerate(("diff20", "opp30", "diff30", "th20"))]
+        diffs = [sb(f"diffs{v}", [P, 2, HS], F32, tag) for v, tag in enumerate(("wq_bf0", "wq_il0"))]
+        ths = []
+        for v in range(2):
+            for s in range(2):
+                t = 2 * v + s
+                nc.vector.tensor_tensor(diffs[v][:, s, :], listed("sec", t, 1), opps[t][:], ALU.subtract)
+            th2 = sb(f"ths{v}", [P, 2, HS], F32)
+            nc.scalar.activation(th2[:], diffs[v][:], ACT.Tanh)
+            ths.extend([th2[:, 0, :], th2[:, 1, :]])
+        own1 = [owns(t, 1, tag) for t, tag in enumerate(("diff20", "opp30", "diff30", "th20"))]
+        wq1 = sb("wq_bf1", [P, PACK, HS], BF16)
+        for t in range(PACK):
+            combine(t, wq1, ths[t], own1[t])
+        dl0a = sb("dl0a", [P, 2, HS], F32, "wq_bf0")
+        nc.scalar.copy(out=dl0a[:], in_=banks0[0][:])
+        place(0, 0, dl0a[:, 0, :], False)
+        place(1, 0, dl0a[:, 1, :], False)
+        dl0b = sb("dl0b", [P, HS], F32, "wq_il0")
+        nc.scalar.copy(out=dl0b[:], in_=banks0[1][:, 0, :])
+        place(2, 0, dl0b[:], False)
+        banks1 = deliver(1, wq1, (3, 0, 1, 2))
+        dl0c = sb("dl0c", [P, HS], F32, "wq_bf1")
+        nc.vector.tensor_copy(out=dl0c[:], in_=banks0[1][:, 1, :])
+        place(3, 0, dl0c[:], True)
+        dl1a = sb("dl1a", [P, 2, HS], F32)
+        nc.scalar.copy(out=dl1a[:], in_=banks1[0][:])
+        place(3, 1, dl1a[:, 0, :], True)
+        place(0, 1, dl1a[:, 1, :], False)
+        dl1b = sb("dl1b", [P, 2, HS], F32)
+        nc.scalar.copy(out=dl1b[:], in_=banks1[1][:])
+        place(1, 1, dl1b[:, 0, :], False)
+        place(2, 1, dl1b[:, 1, :], False)
+        for u in (3, 0, 1, 2):
+            finish(u, 2)

from contextlib import ExitStack

import concourse.mybir as mybir

D, T, I, Q, E, M = 512, 1024, 512, 512, 512, 1024
FLOPS = 2 * D * Q * T + 2 * Q * E * I

F32 = mybir.dt.float32
BF16 = mybir.dt.bfloat16
I32 = mybir.dt.int32
U32 = mybir.dt.uint32
U16 = mybir.dt.uint16
U8 = mybir.dt.uint8
FP8X4 = mybir.dt.float8_e4m3fn_x4
ALU = mybir.AluOpType
ACT = mybir.ActivationFunctionType

P = 128
PACK = 4
BANK = 512
HALVES = 2
HS = I // HALVES
HC = HS // 16


def tile_attend_seconded_deliveredplanes_lean_kernel(
    tc, query, keys_words, keys_scales, lam, qs, msgs, old, offs, offs2, offs3, offs4, out
):
    nc = tc.nc
    with ExitStack() as ctx:
        keep = ctx.enter_context(tc.tile_pool(name="keep", bufs=1))
        psum_a = ctx.enter_context(tc.psum_pool(name="psum_a", bufs=4))
        psum_d = ctx.enter_context(tc.psum_pool(name="psum_d", bufs=4))

        def sb(name, shape, dtype, tag=None):
            return keep.tile(shape, dtype, name=name, tag=tag or name, align_bytes=64)

        lists = {n: keep.tile([P, I // 16], U16, name=n) for n in ("own", "sec", "opp", "dst")}
        q_raw = [sb(f"q_raw{c}", [P, PACK, Q // 2], F32) for c in range(2)]
        k_words = [sb(f"k_words{c}", [P, BANK], U32) for c in range(T // BANK)]
        k_scales = sb("k_scales", [P, T], U8)
        lam_t = sb("lam_t", [P, PACK], F32)
        qs_t = sb("qs_t", [P, PACK], F32)
        m_raw = sb("m_raw", [P, PACK, E], F32)
        old_t = [sb(f"old{u}", [P, M], F32) for u in range(E // P)]
        df = [sb(f"df{u}", [P, M], F32) for u in range(2)]

        q_view = query.rearrange("(p j) q -> p j q", j=PACK)
        for c in range(2):
            nc.sync.dma_start(out=q_raw[c][:], in_=q_view[:, :, c * (Q // 2) : (c + 1) * (Q // 2)])
        nc.scalar.dma_start(out=qs_t[:], in_=qs.rearrange("(p t) o -> p (t o)", t=PACK))
        for g in range(4):
            nc.scalar.dma_start(
                out=k_scales[32 * g : 32 * g + 4, :].bitcast(I32),
                in_=keys_scales[0, 4 * g : 4 * g + 4, :].bitcast(I32),
            )
        kw = keys_words[0].rearrange("p n r -> p (n r)")
        for c in range(T // BANK):
            nc.sync.dma_start(
                out=k_words[c][:].bitcast(I32),
                in_=kw[:, c * BANK * PACK : (c + 1) * BANK * PACK].bitcast(I32),
            )
        nc.gpsimd.dma_start(out=lam_t[:], in_=lam.rearrange("(p t) o -> p (t o)", t=PACK))
        nc.sync.dma_start(lists["opp"][:], offs3)
        nc.sync.dma_start(lists["own"][:], offs)
        nc.sync.dma_start(lists["sec"][:], offs2)
        nc.sync.dma_start(out=m_raw[:], in_=msgs.rearrange("(p j) e -> p j e", j=PACK))
        nc.sync.dma_start(lists["dst"][:], offs4)
        for u in range(E // P):
            nc.sync.dma_start(out=old_t[u][:], in_=old[u * P : (u + 1) * P, :])
        for u in range(2):
            nc.vector.memset(df[u][:].bitcast(I32), 0)

        qs_wide = sb("qs_wide", [P, PACK, HS], F32)
        nc.vector.tensor_copy(out=qs_wide[:], in_=qs_t[:].unsqueeze(2).to_broadcast([P, PACK, HS]))
        lq = sb("lq", [P, PACK], F32)
        nc.gpsimd.tensor_tensor(out=lq[:], in0=lam_t[:], in1=qs_t[:], op=ALU.mult)

        q_bf = [sb(f"q_bf{t}", [P, P, PACK], BF16) for t in range(PACK)]
        for c in range(2):
            for t in range(PACK):
                dst = q_bf[t][:, c * (P // 2) : (c + 1) * (P // 2), :]
                src = q_raw[c][:].rearrange("p j (m t) -> p t m j", t=PACK)[:, t, :, :]
                if t % 2 == 0:
                    nc.vector.tensor_copy(out=dst, in_=src)
                else:
                    nc.scalar.copy(out=dst, in_=src)
        q_codes = [sb(f"q_codes{t}", [P, P], U32) for t in range(PACK)]
        q_scales = [sb(f"q_scales{t}", [P, P], U8) for t in range(PACK)]
        for t in range(PACK):
            nc.vector.quantize_mx(
                out=q_codes[t][:].bitcast(FP8X4),
                scales=q_scales[t][:],
                in_=q_bf[t][:].rearrange("p m j -> p (m j)"),
            )

        a = [sb(f"a{t}", [P, T], F32) for t in range(PACK)]

        def scores(t):
            for c in range(T // BANK):
                cols = slice(c * BANK, (c + 1) * BANK)
                bank = psum_a.tile([P, BANK], F32, name="a_bank")
                nc.tensor.matmul_mx(
                    out=bank[:],
                    lhsT=q_codes[t][:].bitcast(FP8X4),
                    lhsT_scale=q_scales[t][:],
                    rhs=k_words[c][:].bitcast(FP8X4),
                    rhs_scale=k_scales[:, cols],
                    start=True,
                    stop=True,
                )
                if t < 2 and c == 1:
                    nc.vector.tensor_copy(out=a[t][:, cols], in_=bank[:])
                else:
                    nc.scalar.copy(out=a[t][:, cols], in_=bank[:])

        def listed(name, t, h):
            return a[t][:].indirect(lists[name][:, h * HC : (h + 1) * HC])

        def opponents(t, h, tag=None):
            opp = sb(f"opp{t}{h}", [P, HS], F32, tag)
            nc.scalar.activation(opp[:], listed("opp", t, h), ACT.Copy)
            return opp

        def owns(t, h, tag=None):
            own = sb(f"own{t}{h}", [P, HS], F32, tag)
            nc.vector.tensor_tensor(own[:], listed("own", t, h), qs_wide[:, t, :], ALU.mult)
            return own

        def contest(t, h, opp, diff):
            nc.vector.tensor_tensor(diff, listed("sec", t, h), opp[:], ALU.subtract)
            th = sb(f"th{t}{h}", [P, HS], F32)
            nc.scalar.activation(th[:], diff, ACT.Tanh)
            return th

        def combine(t, wq_bf, th, own):
            nc.vector.scalar_tensor_tensor(
                out=wq_bf[:, t, :], in0=th, scalar=lq[:, t : t + 1], in1=own[:], op0=ALU.mult, op1=ALU.add
            )

        m_codes = sb("m_codes", [P, E], U32)
        m_scales = sb("m_scales", [P, E], U8)

        def round_messages(c, tag, on_vector):
            m_bf = sb(f"m_bf{c}", [P, E // 2, PACK], BF16, tag)
            dst = m_bf[:].rearrange("p (c i) j -> p c j i", i=4)
            src = m_raw[:, :, c * (E // 2) : (c + 1) * (E // 2)].rearrange("p j (c i) -> p c j i", i=4)
            if on_vector:
                nc.vector.tensor_copy(out=dst, in_=src)
            else:
                nc.scalar.copy(out=dst, in_=src)
            return m_bf

        def quantise_messages(c, m_bf):
            cols = slice(c * (E // 2), (c + 1) * (E // 2))
            nc.vector.quantize_mx(
                out=m_codes[:, cols].bitcast(FP8X4), scales=m_scales[:, cols], in_=m_bf[:].rearrange("p e j -> p (e j)")
            )

        def deliver(h, wq_bf, order):
            wq_il = sb(f"wq_il{h}", [P, HS, PACK], BF16)
            nc.vector.tensor_copy(
                out=wq_il[:].rearrange("p (c i) t -> p c t i", i=4),
                in_=wq_bf[:].rearrange("p t (c i) -> p c t i", i=4),
            )
            w_codes = sb(f"w_codes{h}", [P, HS], U32)
            w_scales = sb(f"w_scales{h}", [P, HS], U8)
            nc.vector.quantize_mx(
                out=w_codes[:].bitcast(FP8X4), scales=w_scales[:], in_=wq_il[:].rearrange("p i t -> p (i t)")
            )
            banks = []
            for v in range(2):
                bank = psum_d.tile([P, 2, HS], F32, name="d_bank")
                for s in range(2):
                    u = order[2 * v + s]
                    cols = slice(u * P, (u + 1) * P)
                    nc.tensor.matmul_mx(
                        out=bank[:, s, :],
                        lhsT=m_codes[:, cols].bitcast(FP8X4),
                        lhsT_scale=m_scales[:, cols],
                        rhs=w_codes[:].bitcast(FP8X4),
                        rhs_scale=w_scales[:],
                        start=True,
                        stop=True,
                    )
                banks.append(bank)
            return banks

        def place(u, h, src, on_vector):
            window = df[u][:].indirect(lists["dst"][:, h * HC : (h + 1) * HC])
            if on_vector:
                nc.vector.tensor_copy(window, src)
            else:
                nc.scalar.activation(window, src, ACT.Copy)

        def finish(u, pieces):
            for c in range(pieces):
                cols = slice(c * M // pieces, (c + 1) * M // pieces)
                nc.vector.tensor_tensor(out=old_t[u][:, cols], in0=old_t[u][:, cols], in1=df[u][:, cols], op=ALU.add)
                nc.sync.dma_start(out=out[u * P : (u + 1) * P, cols], in_=old_t[u][:, cols])

        wq0 = sb("wq_bf0", [P, PACK, HS], BF16)
        scores(0)
        pending = None
        for t in range(PACK):
            opp = opponents(t, 0)
            own = owns(t, 0)
            if t + 1 < PACK:
                scores(t + 1)
            diff = sb(f"diff{t}0", [P, HS], F32)
            th = contest(t, 0, opp, diff[:])
            if pending is not None:
                combine(t - 1, wq0, *pending)
            pending = (th[:], own)
            if t == 2:
                m_low = round_messages(0, "own10", True)
            if t == 3:
                quantise_messages(0, m_low)
                quantise_messages(1, round_messages(1, "opp20", False))
        combine(PACK - 1, wq0, *pending)
        for c in range(2):
            df.append(sb(f"df{2 + c}", [P, M], F32, f"k_words{c}"))
            nc.gpsimd.memset(df[2 + c][:], 0.0)
        banks0 = deliver(0, wq0, (0, 1, 2, 3))
        opps = [opponents(t, 1, tag) for t, tag in enumerate(("diff20", "opp30", "diff30", "th20"))]
        diffs = [sb(f"diffs{v}", [P, 2, HS], F32, tag) for v, tag in enumerate(("wq_bf0", "wq_il0"))]
        ths = []
        for v in range(2):
            for s in range(2):
                t = 2 * v + s
                nc.vector.tensor_tensor(diffs[v][:, s, :], listed("sec", t, 1), opps[t][:], ALU.subtract)
            th2 = sb(f"ths{v}", [P, 2, HS], F32)
            nc.scalar.activation(th2[:], diffs[v][:], ACT.Tanh)
            ths.extend([th2[:, 0, :], th2[:, 1, :]])
        own1 = [owns(t, 1, tag) for t, tag in enumerate(("diff20", "opp30", "diff30", "th20"))]
        wq1 = sb("wq_bf1", [P, PACK, HS], BF16)
        for t in range(PACK):
            combine(t, wq1, ths[t], own1[t])
        dl0a = sb("dl0a", [P, 2, HS], F32, "wq_bf0")
        nc.scalar.copy(out=dl0a[:], in_=banks0[0][:])
        place(0, 0, dl0a[:, 0, :], False)
        place(1, 0, dl0a[:, 1, :], False)
        dl0b = sb("dl0b", [P, HS], F32, "wq_il0")
        nc.scalar.copy(out=dl0b[:], in_=banks0[1][:, 0, :])
        place(2, 0, dl0b[:], False)
        banks1 = deliver(1, wq1, (3, 0, 1, 2))
        dl0c = sb("dl0c", [P, HS], F32, "wq_bf1")
        nc.vector.tensor_copy(out=dl0c[:], in_=banks0[1][:, 1, :])
        place(3, 0, dl0c[:], True)
        dl1a = sb("dl1a", [P, 2, HS], F32)
        nc.scalar.copy(out=dl1a[:], in_=banks1[0][:])
        place(3, 1, dl1a[:, 0, :], True)
        place(0, 1, dl1a[:, 1, :], False)
        dl1b = sb("dl1b", [P, 2, HS], F32)
        nc.scalar.copy(out=dl1b[:], in_=banks1[1][:])
        place(1, 1, dl1b[:, 0, :], False)
        place(2, 1, dl1b[:, 1, :], False)
        for u in (3, 0, 1, 2):
            finish(u, 2)
